import numpy as np
import ml_dtypes


def mxq(x, axis, fmt="e4m3"):
    dtype, down = {"e4m3": (ml_dtypes.float8_e4m3fn, 7), "e5m2": (ml_dtypes.float8_e5m2, 14)}[fmt]
    v = np.moveaxis(np.asarray(x, np.float32).astype(ml_dtypes.bfloat16).astype(np.float64), axis, -1)
    blocks = v.reshape(v.shape[:-1] + (-1, 32))
    amax = np.abs(blocks).max(-1, keepdims=True)
    byte = np.maximum(np.where(amax > 0, np.frexp(amax)[1] - 1 + 127, 0) - down, 1)
    scale = np.exp2(byte - 127.0)
    codes = (blocks / scale).astype(np.float32).astype(dtype).astype(np.float64)
    return np.moveaxis((codes * scale).reshape(v.shape), -1, axis)


WIDE = False


def mx_kscale(k):
    if not WIDE:
        return np.ones(k)
    levels = np.array([10, -10, 5, -5, 0])
    if k % 512:
        return np.exp2(np.random.permutation(np.resize(levels, k // 32))).repeat(32)
    a = np.empty((k // 512, 16))
    for p in range(k // 512):
        a[p, :8] = np.random.permutation(np.resize(levels, 8))
        for g in range(8):
            far = levels[np.abs(levels - a[p, g]) >= 10]
            a[p, g + 8] = far[np.random.randint(len(far))]
    return np.exp2(a.ravel()).repeat(32)


def f64(x):
    return np.asarray(x).astype(np.float64)


def striped(idx):
    return np.tile(np.asarray(idx).reshape(-1, 16).T, (8, 1)).astype(np.uint16)


def unstriped(offs):
    return offs[:16].T.reshape(-1).astype(np.int64)


E2M1 = np.array([0.0, 0.5, 1.0, 1.5, 2.0, 3.0, 4.0, 6.0, -0.0, -0.5, -1.0, -1.5, -2.0, -3.0, -4.0, -6.0])


def pack_weight(w, fmt):
    k, n = w.shape
    w = f64(np.asarray(w, np.float32).astype(ml_dtypes.bfloat16)).reshape(k // 32, 32, n)
    amax = np.abs(w).max(1)
    if fmt == "e4m3":
        byte = np.frexp(amax)[1] - 1 + 127 - 7
    else:
        mant, ex = np.frexp(amax / 6.0)
        byte = np.where(mant > 0.5, ex, ex - 1) + 127
    byte = np.clip(np.where(amax > 0, byte, 1), 1, 254)
    scaled = (w * np.exp2(127.0 - byte)[:, None, :]).reshape(k, n).astype(np.float32)
    by_word = np.ascontiguousarray(scaled.reshape(k // 512, 128, 4, n).transpose(0, 1, 3, 2))
    if fmt == "e4m3":
        words = by_word.astype(ml_dtypes.float8_e4m3fn).view(np.uint8)
    else:
        c = by_word.astype(ml_dtypes.float4_e2m1fn).view(np.uint8) & 0xF
        words = (c[..., 0::2] | (c[..., 1::2] << 4)).reshape(k // 512, 128, 2 * n)
    return np.ascontiguousarray(words), np.ascontiguousarray(byte.astype(np.uint8).reshape(k // 512, 16, n))


def unpack_weight(words, scales, fmt):
    g, _, n = scales.shape
    words = np.ascontiguousarray(words).reshape(g, 128, n, -1)
    if fmt == "e4m3":
        vals = words.view(ml_dtypes.float8_e4m3fn).astype(np.float64)
    else:
        nib = np.empty((g, 128, n, 4), np.uint8)
        nib[..., 0::2] = words & 0xF
        nib[..., 1::2] = words >> 4
        vals = E2M1[nib]
    vals = vals * np.repeat(np.exp2(scales.astype(np.float64) - 127.0), 8, axis=1)[..., None]
    return vals.transpose(0, 1, 3, 2).reshape(g * 512, n)


D, E, T, I, Q = 512, 512, 2048, 512, 128


def setup_inputs():
    n = np.random.standard_normal
    idx = np.random.permutation(T)[:I]
    fd = mx_kscale(D)
    fe = mx_kscale(E)
    keysp = pack_weight(n((D, T)) / fd[:, None], "e4m3")
    valsp = pack_weight(n((E, T)) / fe[:, None], "e4m3")
    return {
        "query": (n((D, Q)) * 0.4 / np.sqrt(D) * fd[:, None]).astype(np.float32),
        "query2": (n((D, Q)) * 0.6 / np.sqrt(D) * fd[:, None]).astype(np.float32),
        "keys_words": keysp[0],
        "keys_scales": keysp[1],
        "l1": (np.random.uniform(6.2, 6.5, (Q, 1))).astype(np.float32),
        "l2": (np.random.uniform(6.2, 6.5, (Q, 1))).astype(np.float32),
        "floor": (np.random.uniform(0.0005, 0.002, (Q, 1))).astype(np.float32),
        "gout": (n((E, Q)) * 1 / np.sqrt(E) * fe[:, None]).astype(np.float32),
        "vals_words": valsp[0],
        "vals_scales": valsp[1],
        "size": (np.random.uniform(0.5, 2.0, (1, I))).astype(np.float32),
        "old": (0.5 * n((Q, T))).astype(np.float32),
        "offs": striped(idx),
    }


def reference(query, query2, keys_words, keys_scales, l1, l2, floor, gout, vals_words, vals_scales, size, old, offs):
    idx = unstriped(offs)
    keysu = unpack_weight(keys_words, keys_scales, "e4m3")
    valsu = unpack_weight(vals_words, vals_scales, "e4m3")
    queryq = mxq(f64(query), 0, "e4m3")
    keysidxg = keysu[:, idx]
    a = queryq.T @ keysidxg
    query2q = mxq(f64(query2), 0, "e4m3")
    b = query2q.T @ keysidxg
    pa = np.exp(a - f64(l1))
    pb = np.exp(b - f64(l2))
    goutq = mxq(f64(gout), 0, "e4m3")
    valsidxg = valsu[:, idx]
    c0 = goutq.T @ valsidxg
    dpb = c0 * f64(size) * pa / np.square(pb + f64(floor)) * (-1.0)
    db = dpb * pb
    gs = db * 4.0
    gf = np.zeros((Q, T))
    gf[:, idx] = gs
    y = f64(old) + gf
    return y

@@ -1,0 +1,171 @@
+from contextlib import ExitStack
+
+import concourse.mybir as mybir
+from concourse.masks import make_identity
+
+D, E, T, I, Q = 512, 512, 2048, 512, 128
+FLOPS = 3 * 2 * D * I * Q
+
+F32 = mybir.dt.float32
+BF16 = mybir.dt.bfloat16
+I32 = mybir.dt.int32
+U32 = mybir.dt.uint32
+U16 = mybir.dt.uint16
+U8 = mybir.dt.uint8
+FP8X4 = mybir.dt.float8_e4m3fn_x4
+ACT = mybir.ActivationFunctionType
+MULT = mybir.AluOpType.mult
+ADD = mybir.AluOpType.add
+
+P = 128
+PACK = 4
+HALF = I // 2
+VAL_ROW = 4
+STORE_COLS = (256, 512, 512, 512, 256)
+
+
+def tile_attend_bclippedratio_b_s_kernel(
+    tc, query, query2, keys_words, keys_scales, l1, l2, floor, gout, vals_words, vals_scales, size, old, offs, out
+):
+    nc = tc.nc
+    with ExitStack() as ctx:
+        keep = ctx.enter_context(tc.tile_pool(name="keep", bufs=1))
+        share = ctx.enter_context(tc.tile_pool(name="share", bufs=1))
+        psum = ctx.enter_context(tc.psum_pool(name="psum", bufs=1))
+
+        def load_scale_rows(engine, window, scales, row0):
+            by_row = scales[0].rearrange("(g r) t -> r g t", r=PACK)
+            for r in range(PACK):
+                engine.dma_start(out=window[row0 + r : P : 32, :].bitcast(I32), in_=by_row[r].bitcast(I32))
+
+        def load_words(window, words):
+            nc.sync.dma_start(out=window[:].bitcast(I32), in_=words[0].rearrange("p t r -> p (t r)").bitcast(I32))
+
+        def load_rows(raw, x):
+            nc.sync.dma_start(out=raw[:], in_=x.rearrange("(p j) q -> p j q", j=PACK))
+
+        def quantize(name, grouped):
+            codes = keep.tile([P, Q], U32, name=name + "_codes", align_bytes=64)
+            plane = keep.tile([P, Q], U8, name=name + "_plane", align_bytes=64)
+            nc.vector.quantize_mx(
+                out=codes[:].bitcast(FP8X4), scales=plane[:], in_=grouped[:].rearrange("p q j -> p (q j)")
+            )
+            return codes, plane
+
+        offsets = keep.tile([P, I // 16], U16, name="offsets")
+        key_scale_win = share.tile([P, T], U8, name="key_scale_win", offset=1024)
+        val_scale_win = keep.tile([P, T], U8, name="val_scale_win")
+        key_win = keep.tile([P, T], U32, name="key_win", tag="key_then_old")
+        scattered = keep.tile([P, T], F32, name="scattered")
+        q1_raw = keep.tile([P, PACK, Q], F32, name="q1_raw")
+        q2_raw = keep.tile([P, PACK, Q], F32, name="q2_raw")
+
+        ident = keep.tile([P, P], F32, name="ident")
+        make_identity(nc, ident[:])
+        nc.vector.memset(key_scale_win[:].bitcast(I32), 0)
+        nc.vector.memset(val_scale_win[:].bitcast(I32), 0)
+        nc.sync.dma_start(offsets[:], offs)
+        load_words(key_win, keys_words)
+        load_rows(q1_raw, query)
+        load_rows(q2_raw, query2)
+        load_scale_rows(nc.scalar, key_scale_win, keys_scales, 0)
+        load_scale_rows(nc.gpsimd, val_scale_win, vals_scales, VAL_ROW)
+
+        l1_col = keep.tile([P, 1], F32, name="l1_col")
+        l2_col = keep.tile([P, 1], F32, name="l2_col")
+        floor_col = keep.tile([P, 1], F32, name="floor_col")
+        size_cols = keep.tile([P, PACK], F32, name="size_cols")
+        nc.gpsimd.dma_start(out=l1_col[:], in_=l1)
+        nc.gpsimd.dma_start(out=size_cols[:], in_=size.rearrange("o (p j) -> (o p) j", j=PACK))
+        nc.gpsimd.dma_start(out=l2_col[:], in_=l2)
+        nc.gpsimd.dma_start(out=floor_col[:], in_=floor)
+        nc.vector.memset(scattered[:], 0.0)
+
+        key_plane = keep.tile([P, I], U8, name="key_plane", align_bytes=64)
+        key_codes = keep.tile([P, I], U32, name="key_codes", align_bytes=64)
+        nc.vector.tensor_copy(key_plane[:], key_scale_win[:].indirect(offsets[:]))
+
+        gout_raw = share.tile([P, PACK, Q], F32, name="gout_raw", offset=0)
+        val_win = share.tile([P, T], U32, name="val_win", offset=2048)
+        load_rows(gout_raw, gout)
+        load_words(val_win, vals_words)
+
+        nc.vector.tensor_copy(key_codes[:], key_win[:].indirect(offsets[:]))
+        old_sb = keep.tile([P, T], F32, name="old_sb", tag="key_then_old")
+        nc.sync.dma_start(out=old_sb[:], in_=old)
+
+        neg_l1 = keep.tile([P, 1], F32, name="neg_l1")
+        neg_l2 = keep.tile([P, 1], F32, name="neg_l2")
+        nc.vector.tensor_scalar_mul(neg_l1[:], l1_col[:], -1.0)
+        nc.vector.tensor_scalar_mul(neg_l2[:], l2_col[:], -1.0)
+
+        q1_grp = keep.tile([P, Q, PACK], BF16, name="q1_grp", align_bytes=64)
+        q2_grp = keep.tile([P, Q, PACK], BF16, name="q2_grp", align_bytes=64)
+        gout_grp = keep.tile([P, Q, PACK], BF16, name="gout_grp", align_bytes=64)
+        nc.scalar.copy(out=q1_grp[:], in_=q1_raw[:].rearrange("p j q -> p q j"))
+        nc.scalar.copy(out=q2_grp[:], in_=q2_raw[:].rearrange("p j q -> p q j"))
+        q1_codes, q1_plane = quantize("q1", q1_grp)
+        q2_codes, q2_plane = quantize("q2", q2_grp)
+
+        a_ps = psum.tile([P, I], F32, name="a_ps")
+        b_ps = psum.tile([P, I], F32, name="b_ps")
+        for ps, codes, plane in ((a_ps, q1_codes, q1_plane), (b_ps, q2_codes, q2_plane)):
+            nc.tensor.matmul_mx(
+                out=ps[:], lhsT=codes[:].bitcast(FP8X4), lhsT_scale=plane[:],
+                rhs=key_codes[:].bitcast(FP8X4), rhs_scale=key_plane[:], start=True, stop=True,
+            )
+        size_ps = psum.tile([P, PACK, P], F32, name="size_ps")
+        for j in range(PACK):
+            nc.tensor.transpose(size_ps[:, j, :], size_cols[:, j : j + 1].to_broadcast([P, P]), ident[:])
+
+        pa = keep.tile([P, I], F32, name="pa")
+        pb = keep.tile([P, I], F32, name="pb")
+        nc.scalar.activation(out=pa[:], in_=a_ps[:], func=ACT.Exp, bias=neg_l1[:], scale=1.0)
+        nc.scalar.activation(out=pb[:], in_=b_ps[:], func=ACT.Exp, bias=neg_l2[:], scale=1.0)
+
+        nc.vector.tensor_copy(out=gout_grp[:], in_=gout_raw[:].rearrange("p j q -> p q j"))
+        val_plane = keep.tile([P, I], U8, name="val_plane", align_bytes=64)
+        nc.vector.tensor_copy(val_plane[:], val_scale_win[:].indirect(offsets[:]))
+        gout_codes, gout_plane = quantize("gout", gout_grp)
+
+        sized = keep.tile([P, I], F32, name="sized")
+        numer = keep.tile([P, I], F32, name="numer")
+        nc.vector.scalar_tensor_tensor(
+            out=sized[:].rearrange("p (n j) -> p n j", j=PACK), in0=pa[:].rearrange("p (n j) -> p n j", j=PACK),
+            scalar=-4.0, in1=size_ps[:].rearrange("p j n -> p n j"), op0=MULT, op1=MULT,
+        )
+        nc.vector.tensor_tensor(numer[:], sized[:], pb[:], MULT)
+
+        halves = [slice(h * HALF, (h + 1) * HALF) for h in range(2)]
+        lists = [offsets[:, h * HALF // 16 : (h + 1) * HALF // 16] for h in range(2)]
+        inv_sq = []
+        for h, cols in enumerate(halves):
+            root = keep.tile([P, HALF], F32, name=f"root{h}")
+            inv = keep.tile([P, HALF], F32, name=f"inv{h}")
+            inv2 = keep.tile([P, HALF], F32, name=f"inv_sq{h}")
+            nc.scalar.activation(out=root[:], in_=pb[:, cols], func=ACT.Abs_reciprocal_sqrt, bias=floor_col[:], scale=1.0)
+            nc.scalar.activation(out=inv[:], in_=root[:], func=ACT.Square)
+            nc.scalar.activation(out=inv2[:], in_=inv[:], func=ACT.Square)
+            inv_sq.append(inv2)
+
+        c_ps = []
+        for h, cols in enumerate(halves):
+            val_codes = keep.tile([P, HALF], U32, name=f"val_codes{h}", align_bytes=64)
+            nc.vector.tensor_copy(val_codes[:], val_win[:].indirect(lists[h]))
+            bank = psum.tile([P, HALF], F32, name=f"c_ps{h}")
+            nc.tensor.matmul_mx(
+                out=bank[:], lhsT=gout_codes[:].bitcast(FP8X4), lhsT_scale=gout_plane[:],
+                rhs=val_codes[:].bitcast(FP8X4), rhs_scale=val_plane[VAL_ROW:P, cols], start=True, stop=True,
+            )
+            c_ps.append(bank)
+        for h, cols in enumerate(halves):
+            grad = keep.tile([P, HALF], F32, name=f"grad{h}")
+            nc.vector.tensor_tensor(grad[:], c_ps[h][:], numer[:, cols], MULT)
+            nc.vector.tensor_tensor(scattered[:].indirect(lists[h]), grad[:], inv_sq[h][:], MULT)
+
+        c0 = 0
+        for width in STORE_COLS:
+            cols = slice(c0, c0 + width)
+            nc.vector.tensor_tensor(old_sb[:, cols], old_sb[:, cols], scattered[:, cols], ADD)
+            nc.sync.dma_start(out=out[:, cols], in_=old_sb[:, cols])
+            c0 = c0 + width

@@ -30,7 +30,6 @@ def tile_attend_bclippedratio_b_s_kernel(
     nc = tc.nc
     with ExitStack() as ctx:
         keep = ctx.enter_context(tc.tile_pool(name="keep", bufs=1))
-        share = ctx.enter_context(tc.tile_pool(name="share", bufs=1))
         psum = ctx.enter_context(tc.psum_pool(name="psum", bufs=1))
 
         def load_scale_rows(engine, window, scales, row0):
@@ -53,51 +52,48 @@ def tile_attend_bclippedratio_b_s_kernel(
             return codes, plane
 
         offsets = keep.tile([P, I // 16], U16, name="offsets")
-        key_scale_win = share.tile([P, T], U8, name="key_scale_win", offset=1024)
+        key_scale_win = keep.tile([P, T], U8, name="key_scale_win")
         val_scale_win = keep.tile([P, T], U8, name="val_scale_win")
-        key_win = keep.tile([P, T], U32, name="key_win", tag="key_then_old")
+        key_win = keep.tile([P, T], U32, name="key_win")
+        val_win = keep.tile([P, T], U32, name="val_win")
         scattered = keep.tile([P, T], F32, name="scattered")
+        old_sb = keep.tile([P, T], F32, name="old_sb")
         q1_raw = keep.tile([P, PACK, Q], F32, name="q1_raw")
         q2_raw = keep.tile([P, PACK, Q], F32, name="q2_raw")
-
-        ident = keep.tile([P, P], F32, name="ident")
-        make_identity(nc, ident[:])
-        nc.vector.memset(key_scale_win[:].bitcast(I32), 0)
-        nc.vector.memset(val_scale_win[:].bitcast(I32), 0)
-        nc.sync.dma_start(offsets[:], offs)
-        load_words(key_win, keys_words)
-        load_rows(q1_raw, query)
-        load_rows(q2_raw, query2)
-        load_scale_rows(nc.scalar, key_scale_win, keys_scales, 0)
-        load_scale_rows(nc.gpsimd, val_scale_win, vals_scales, VAL_ROW)
-
+        gout_raw = keep.tile([P, PACK, Q], F32, name="gout_raw")
         l1_col = keep.tile([P, 1], F32, name="l1_col")
         l2_col = keep.tile([P, 1], F32, name="l2_col")
         floor_col = keep.tile([P, 1], F32, name="floor_col")
         size_cols = keep.tile([P, PACK], F32, name="size_cols")
-        nc.gpsimd.dma_start(out=l1_col[:], in_=l1)
-        nc.gpsimd.dma_start(out=size_cols[:], in_=size.rearrange("o (p j) -> (o p) j", j=PACK))
-        nc.gpsimd.dma_start(out=l2_col[:], in_=l2)
-        nc.gpsimd.dma_start(out=floor_col[:], in_=floor)
+        ident = keep.tile([P, P], F32, name="ident")
+
+        nc.vector.memset(key_scale_win[:].bitcast(I32), 0)
         nc.vector.memset(scattered[:], 0.0)
+        nc.vector.memset(val_scale_win[:].bitcast(I32), 0)
+        nc.sync.dma_start(offsets[:], offs)
+        nc.sync.dma_start(out=l1_col[:], in_=l1)
+        nc.sync.dma_start(out=l2_col[:], in_=l2)
+        load_words(key_win, keys_words)
+        load_scale_rows(nc.scalar, key_scale_win, keys_scales, 0)
+        load_rows(q1_raw, query)
+        load_rows(q2_raw, query2)
+        load_rows(gout_raw, gout)
+        load_words(val_win, vals_words)
+        load_scale_rows(nc.scalar, val_scale_win, vals_scales, VAL_ROW)
+        nc.sync.dma_start(out=floor_col[:], in_=floor)
+        nc.sync.dma_start(out=old_sb[:], in_=old)
+        make_identity(nc, ident[:])
+        nc.gpsimd.dma_start(out=size_cols[:], in_=size.rearrange("o (p j) -> (o p) j", j=PACK))
 
         key_plane = keep.tile([P, I], U8, name="key_plane", align_bytes=64)
         key_codes = keep.tile([P, I], U32, name="key_codes", align_bytes=64)
         nc.vector.tensor_copy(key_plane[:], key_scale_win[:].indirect(offsets[:]))
-
-        gout_raw = share.tile([P, PACK, Q], F32, name="gout_raw", offset=0)
-        val_win = share.tile([P, T], U32, name="val_win", offset=2048)
-        load_rows(gout_raw, gout)
-        load_words(val_win, vals_words)
-
         nc.vector.tensor_copy(key_codes[:], key_win[:].indirect(offsets[:]))
-        old_sb = keep.tile([P, T], F32, name="old_sb", tag="key_then_old")
-        nc.sync.dma_start(out=old_sb[:], in_=old)
 
         neg_l1 = keep.tile([P, 1], F32, name="neg_l1")
         neg_l2 = keep.tile([P, 1], F32, name="neg_l2")
-        nc.vector.tensor_scalar_mul(neg_l1[:], l1_col[:], -1.0)
-        nc.vector.tensor_scalar_mul(neg_l2[:], l2_col[:], -1.0)
+        nc.scalar.activation(out=neg_l1[:], in_=l1_col[:], func=ACT.Copy, scale=-1.0)
+        nc.scalar.activation(out=neg_l2[:], in_=l2_col[:], func=ACT.Copy, scale=-1.0)
 
         q1_grp = keep.tile([P, Q, PACK], BF16, name="q1_grp", align_bytes=64)
         q2_grp = keep.tile([P, Q, PACK], BF16, name="q2_grp", align_bytes=64)

from contextlib import ExitStack

import concourse.mybir as mybir
from concourse.masks import make_identity

D, E, T, I, Q = 512, 512, 2048, 512, 128
FLOPS = 3 * 2 * D * I * Q

F32 = mybir.dt.float32
BF16 = mybir.dt.bfloat16
I32 = mybir.dt.int32
U32 = mybir.dt.uint32
U16 = mybir.dt.uint16
U8 = mybir.dt.uint8
FP8X4 = mybir.dt.float8_e4m3fn_x4
ACT = mybir.ActivationFunctionType
MULT = mybir.AluOpType.mult
ADD = mybir.AluOpType.add

P = 128
PACK = 4
HALF = I // 2
VAL_ROW = 4
STORE_COLS = (256, 512, 512, 512, 256)


def tile_attend_bclippedratio_b_s_kernel(
    tc, query, query2, keys_words, keys_scales, l1, l2, floor, gout, vals_words, vals_scales, size, old, offs, out
):
    nc = tc.nc
    with ExitStack() as ctx:
        keep = ctx.enter_context(tc.tile_pool(name="keep", bufs=1))
        psum = ctx.enter_context(tc.psum_pool(name="psum", bufs=1))

        def load_scale_rows(engine, window, scales, row0):
            by_row = scales[0].rearrange("(g r) t -> r g t", r=PACK)
            for r in range(PACK):
                engine.dma_start(out=window[row0 + r : P : 32, :].bitcast(I32), in_=by_row[r].bitcast(I32))

        def load_words(window, words):
            nc.sync.dma_start(out=window[:].bitcast(I32), in_=words[0].rearrange("p t r -> p (t r)").bitcast(I32))

        def load_rows(raw, x):
            nc.sync.dma_start(out=raw[:], in_=x.rearrange("(p j) q -> p j q", j=PACK))

        def quantize(name, grouped):
            codes = keep.tile([P, Q], U32, name=name + "_codes", align_bytes=64)
            plane = keep.tile([P, Q], U8, name=name + "_plane", align_bytes=64)
            nc.vector.quantize_mx(
                out=codes[:].bitcast(FP8X4), scales=plane[:], in_=grouped[:].rearrange("p q j -> p (q j)")
            )
            return codes, plane

        offsets = keep.tile([P, I // 16], U16, name="offsets")
        key_scale_win = keep.tile([P, T], U8, name="key_scale_win")
        val_scale_win = keep.tile([P, T], U8, name="val_scale_win")
        key_win = keep.tile([P, T], U32, name="key_win")
        val_win = keep.tile([P, T], U32, name="val_win")
        scattered = keep.tile([P, T], F32, name="scattered")
        old_sb = keep.tile([P, T], F32, name="old_sb")
        q1_raw = keep.tile([P, PACK, Q], F32, name="q1_raw")
        q2_raw = keep.tile([P, PACK, Q], F32, name="q2_raw")
        gout_raw = keep.tile([P, PACK, Q], F32, name="gout_raw")
        l1_col = keep.tile([P, 1], F32, name="l1_col")
        l2_col = keep.tile([P, 1], F32, name="l2_col")
        floor_col = keep.tile([P, 1], F32, name="floor_col")
        size_cols = keep.tile([P, PACK], F32, name="size_cols")
        ident = keep.tile([P, P], F32, name="ident")

        nc.vector.memset(key_scale_win[:].bitcast(I32), 0)
        nc.vector.memset(scattered[:], 0.0)
        nc.vector.memset(val_scale_win[:].bitcast(I32), 0)
        nc.sync.dma_start(offsets[:], offs)
        nc.sync.dma_start(out=l1_col[:], in_=l1)
        nc.sync.dma_start(out=l2_col[:], in_=l2)
        load_words(key_win, keys_words)
        load_scale_rows(nc.scalar, key_scale_win, keys_scales, 0)
        load_rows(q1_raw, query)
        load_rows(q2_raw, query2)
        load_rows(gout_raw, gout)
        load_words(val_win, vals_words)
        load_scale_rows(nc.scalar, val_scale_win, vals_scales, VAL_ROW)
        nc.sync.dma_start(out=floor_col[:], in_=floor)
        nc.sync.dma_start(out=old_sb[:], in_=old)
        make_identity(nc, ident[:])
        nc.gpsimd.dma_start(out=size_cols[:], in_=size.rearrange("o (p j) -> (o p) j", j=PACK))

        key_plane = keep.tile([P, I], U8, name="key_plane", align_bytes=64)
        key_codes = keep.tile([P, I], U32, name="key_codes", align_bytes=64)
        nc.vector.tensor_copy(key_plane[:], key_scale_win[:].indirect(offsets[:]))
        nc.vector.tensor_copy(key_codes[:], key_win[:].indirect(offsets[:]))

        neg_l1 = keep.tile([P, 1], F32, name="neg_l1")
        neg_l2 = keep.tile([P, 1], F32, name="neg_l2")
        nc.scalar.activation(out=neg_l1[:], in_=l1_col[:], func=ACT.Copy, scale=-1.0)
        nc.scalar.activation(out=neg_l2[:], in_=l2_col[:], func=ACT.Copy, scale=-1.0)

        q1_grp = keep.tile([P, Q, PACK], BF16, name="q1_grp", align_bytes=64)
        q2_grp = keep.tile([P, Q, PACK], BF16, name="q2_grp", align_bytes=64)
        gout_grp = keep.tile([P, Q, PACK], BF16, name="gout_grp", align_bytes=64)
        nc.scalar.copy(out=q1_grp[:], in_=q1_raw[:].rearrange("p j q -> p q j"))
        nc.scalar.copy(out=q2_grp[:], in_=q2_raw[:].rearrange("p j q -> p q j"))
        q1_codes, q1_plane = quantize("q1", q1_grp)
        q2_codes, q2_plane = quantize("q2", q2_grp)

        a_ps = psum.tile([P, I], F32, name="a_ps")
        b_ps = psum.tile([P, I], F32, name="b_ps")
        for ps, codes, plane in ((a_ps, q1_codes, q1_plane), (b_ps, q2_codes, q2_plane)):
            nc.tensor.matmul_mx(
                out=ps[:], lhsT=codes[:].bitcast(FP8X4), lhsT_scale=plane[:],
                rhs=key_codes[:].bitcast(FP8X4), rhs_scale=key_plane[:], start=True, stop=True,
            )
        size_ps = psum.tile([P, PACK, P], F32, name="size_ps")
        for j in range(PACK):
            nc.tensor.transpose(size_ps[:, j, :], size_cols[:, j : j + 1].to_broadcast([P, P]), ident[:])

        pa = keep.tile([P, I], F32, name="pa")
        pb = keep.tile([P, I], F32, name="pb")
        nc.scalar.activation(out=pa[:], in_=a_ps[:], func=ACT.Exp, bias=neg_l1[:], scale=1.0)
        nc.scalar.activation(out=pb[:], in_=b_ps[:], func=ACT.Exp, bias=neg_l2[:], scale=1.0)

        nc.vector.tensor_copy(out=gout_grp[:], in_=gout_raw[:].rearrange("p j q -> p q j"))
        val_plane = keep.tile([P, I], U8, name="val_plane", align_bytes=64)
        nc.vector.tensor_copy(val_plane[:], val_scale_win[:].indirect(offsets[:]))
        gout_codes, gout_plane = quantize("gout", gout_grp)

        sized = keep.tile([P, I], F32, name="sized")
        numer = keep.tile([P, I], F32, name="numer")
        nc.vector.scalar_tensor_tensor(
            out=sized[:].rearrange("p (n j) -> p n j", j=PACK), in0=pa[:].rearrange("p (n j) -> p n j", j=PACK),
            scalar=-4.0, in1=size_ps[:].rearrange("p j n -> p n j"), op0=MULT, op1=MULT,
        )
        nc.vector.tensor_tensor(numer[:], sized[:], pb[:], MULT)

        halves = [slice(h * HALF, (h + 1) * HALF) for h in range(2)]
        lists = [offsets[:, h * HALF // 16 : (h + 1) * HALF // 16] for h in range(2)]
        inv_sq = []
        for h, cols in enumerate(halves):
            root = keep.tile([P, HALF], F32, name=f"root{h}")
            inv = keep.tile([P, HALF], F32, name=f"inv{h}")
            inv2 = keep.tile([P, HALF], F32, name=f"inv_sq{h}")
            nc.scalar.activation(out=root[:], in_=pb[:, cols], func=ACT.Abs_reciprocal_sqrt, bias=floor_col[:], scale=1.0)
            nc.scalar.activation(out=inv[:], in_=root[:], func=ACT.Square)
            nc.scalar.activation(out=inv2[:], in_=inv[:], func=ACT.Square)
            inv_sq.append(inv2)

        c_ps = []
        for h, cols in enumerate(halves):
            val_codes = keep.tile([P, HALF], U32, name=f"val_codes{h}", align_bytes=64)
            nc.vector.tensor_copy(val_codes[:], val_win[:].indirect(lists[h]))
            bank = psum.tile([P, HALF], F32, name=f"c_ps{h}")
            nc.tensor.matmul_mx(
                out=bank[:], lhsT=gout_codes[:].bitcast(FP8X4), lhsT_scale=gout_plane[:],
                rhs=val_codes[:].bitcast(FP8X4), rhs_scale=val_plane[VAL_ROW:P, cols], start=True, stop=True,
            )
            c_ps.append(bank)
        for h, cols in enumerate(halves):
            grad = keep.tile([P, HALF], F32, name=f"grad{h}")
            nc.vector.tensor_tensor(grad[:], c_ps[h][:], numer[:, cols], MULT)
            nc.vector.tensor_tensor(scattered[:].indirect(lists[h]), grad[:], inv_sq[h][:], MULT)

        c0 = 0
        for width in STORE_COLS:
            cols = slice(c0, c0 + width)
            nc.vector.tensor_tensor(old_sb[:, cols], old_sb[:, cols], scattered[:, cols], ADD)
            nc.sync.dma_start(out=out[:, cols], in_=old_sb[:, cols])
            c0 = c0 + width
